import numpy as np
import ml_dtypes


def mxq(x, axis, fmt="e4m3"):
    dtype, down = {"e4m3": (ml_dtypes.float8_e4m3fn, 7), "e5m2": (ml_dtypes.float8_e5m2, 14)}[fmt]
    v = np.moveaxis(np.asarray(x, np.float32).astype(ml_dtypes.bfloat16).astype(np.float64), axis, -1)
    blocks = v.reshape(v.shape[:-1] + (-1, 32))
    amax = np.abs(blocks).max(-1, keepdims=True)
    byte = np.maximum(np.where(amax > 0, np.frexp(amax)[1] - 1 + 127, 0) - down, 1)
    scale = np.exp2(byte - 127.0)
    codes = (blocks / scale).astype(np.float32).astype(dtype).astype(np.float64)
    return np.moveaxis((codes * scale).reshape(v.shape), -1, axis)


WIDE = False


def mx_kscale(k):
    if not WIDE:
        return np.ones(k)
    levels = np.array([10, -10, 5, -5, 0])
    if k % 512:
        return np.exp2(np.random.permutation(np.resize(levels, k // 32))).repeat(32)
    a = np.empty((k // 512, 16))
    for p in range(k // 512):
        a[p, :8] = np.random.permutation(np.resize(levels, 8))
        for g in range(8):
            far = levels[np.abs(levels - a[p, g]) >= 10]
            a[p, g + 8] = far[np.random.randint(len(far))]
    return np.exp2(a.ravel()).repeat(32)


def f64(x):
    return np.asarray(x).astype(np.float64)


def striped(idx):
    return np.tile(idx.reshape(-1, 16).T, (8, 1)).astype(np.uint16)


def unstriped(offs):
    return offs[:16].T.reshape(-1).astype(np.int64)


def pack_weight(w):
    k, n = w.shape
    w = f64(np.asarray(w, np.float32).astype(ml_dtypes.bfloat16)).reshape(k // 32, 32, n)
    amax = np.abs(w).max(1)
    byte = np.clip(np.where(amax > 0, np.frexp(amax)[1] - 1 + 127 - 7, 1), 1, 254)
    scaled = (w * np.exp2(127.0 - byte)[:, None, :]).reshape(k, n).astype(np.float32)
    words = np.ascontiguousarray(scaled.reshape(k // 512, 128, 4, n).transpose(0, 1, 3, 2)).astype(ml_dtypes.float8_e4m3fn).view(np.uint8)
    return words, np.ascontiguousarray(byte.astype(np.uint8).reshape(k // 512, 16, n))


def unpack_weight(words, scales):
    g, p, n, _ = words.shape
    vals = np.ascontiguousarray(words).view(ml_dtypes.float8_e4m3fn).astype(np.float64) * np.repeat(np.exp2(scales.astype(np.float64) - 127.0), 8, axis=1)[..., None]
    return vals.transpose(0, 1, 3, 2).reshape(g * 512, n)


K, T, S, N, V, R = 512, 1024, 512, 256, 256, 128


def setup_inputs():
    n = np.random.standard_normal
    s = mx_kscale(K)[:, None]
    packed_xT = pack_weight(n((K, T)) * s)
    return {
        "x_words": packed_xT[0],
        "x_scales": packed_xT[1],
        "w1": (n((K, N)) / np.sqrt(K) / s).astype(np.float32),
        "offs": striped(np.random.permutation(T)[:S]),
        "ea": striped(np.random.randint(0, S, V)),
        "eb": striped(np.random.randint(0, S, V)),
        "wa": striped(np.random.randint(0, S, V)),
        "wb": striped(np.random.randint(0, S, V)),
        "cen": striped(np.random.permutation(S)[:R]),
        "i1": striped(np.random.permutation(V)[:R]),
        "i2": striped(np.random.permutation(V)[:R]),
    }


def reference(x_words, x_scales, w1, offs, ea, eb, wa, wb, cen, i1, i2):
    xq = unpack_weight(x_words, x_scales)[:, unstriped(offs)]
    y = mxq(f64(w1), 0, "e4m3").T @ xq
    edge = 0.375 * (y[:, unstriped(ea)] + y[:, unstriped(eb)]) + 0.125 * (y[:, unstriped(wa)] + y[:, unstriped(wb)])
    return 0.4 * y[:, unstriped(cen)] + 0.3 * (edge[:, unstriped(i1)] + edge[:, unstriped(i2)])

@@ -1,0 +1,160 @@
+from contextlib import ExitStack
+
+import concourse.mybir as mybir
+
+K, T, S, N, V, R = 512, 1024, 512, 256, 256, 128
+FLOPS = 2 * K * N * S
+
+F32 = mybir.dt.float32
+BF16 = mybir.dt.bfloat16
+I32 = mybir.dt.int32
+U32 = mybir.dt.uint32
+U16 = mybir.dt.uint16
+U8 = mybir.dt.uint8
+FP8X4 = mybir.dt.float8_e4m3fn_x4
+ADD = mybir.AluOpType.add
+MULT = mybir.AluOpType.mult
+COPY = mybir.ActivationFunctionType.Copy
+
+P = 128
+PACK = 4
+BLOCKS = N // P
+HALF = S // 2
+WING = 0.3 * 0.125
+END_TO_WING = 0.375 / 0.125
+OWN_TO_WING = 0.4 / WING
+
+
+def tile_picked_yloopsd_one_p_kernel(
+    tc, x_words, x_scales, w1, offs, ea, eb, wa, wb, cen, i1, i2, out
+):
+    nc = tc.nc
+    with ExitStack() as ctx:
+        held = ctx.enter_context(tc.tile_pool(name="held", bufs=1))
+        psum = ctx.enter_context(tc.psum_pool(name="psum", bufs=1))
+
+        def load_list(name, source):
+            tile = held.tile([P, source.shape[1]], U16, name=name)
+            nc.sync.dma_start(tile[:], source)
+            return tile
+
+        table_scales = held.tile([P, T], U8, align_bytes=64)
+        offs_t = load_list("offs_t", offs)
+        for q in range(4):
+            (nc.sync if q < 2 else nc.scalar).dma_start(
+                table_scales[32 * q : 32 * q + 32, :].bitcast(I32),
+                x_scales[0, 4 * q : 4 * q + 4, :].bitcast(I32).unsqueeze(0).to_broadcast([8, 4, T // 4]),
+            )
+        w_rows = w1.rearrange("(p j) n -> p j n", j=PACK)
+        w_raw = [held.tile([P, PACK, P], F32, name=f"w_raw{b}", align_bytes=64) for b in range(BLOCKS)]
+        nc.sync.dma_start(w_raw[0][:], w_rows[:, :, 0:P])
+        table_words = held.tile([P, T], U32, align_bytes=64)
+        nc.sync.dma_start(
+            table_words[:].bitcast(I32), x_words[0].rearrange("p n t -> p (n t)").bitcast(I32)
+        )
+        nc.sync.dma_start(w_raw[1][:], w_rows[:, :, P : 2 * P])
+        ea_t = load_list("ea_t", ea)
+        wa_t = load_list("wa_t", wa)
+        eb_t = load_list("eb_t", eb)
+        wb_t = load_list("wb_t", wb)
+        cen_t = load_list("cen_t", cen)
+        i1_t = load_list("i1_t", i1)
+        i2_t = load_list("i2_t", i2)
+
+        x_s = held.tile([P, S], U8, align_bytes=64)
+        x_c = held.tile([P, S], U32, align_bytes=64)
+        w_bf = [held.tile([P, P, PACK], BF16, name=f"w_bf{b}", align_bytes=64) for b in range(BLOCKS)]
+        w_c = [held.tile([P, P], U32, name=f"w_c{b}", align_bytes=64) for b in range(BLOCKS)]
+        w_s = [held.tile([P, P], U8, name=f"w_s{b}", align_bytes=64) for b in range(BLOCKS)]
+        y = [held.tile([P, S], F32, name=f"y{b}") for b in range(BLOCKS)]
+
+        def cast(b):
+            nc.scalar.activation(
+                w_bf[b][:], w_raw[b][:].rearrange("p j n -> p n j"), COPY
+            )
+
+        def quantize(b):
+            nc.vector.quantize_mx(
+                out=w_c[b][:].bitcast(FP8X4),
+                scales=w_s[b][:],
+                in_=w_bf[b][:].rearrange("p n j -> p (n j)"),
+            )
+
+        def pick_words(h):
+            cols = slice(h * HALF, (h + 1) * HALF)
+            nc.vector.tensor_copy(
+                x_c[:, cols], table_words[:].indirect(offs_t[:, h * HALF // 16 : (h + 1) * HALF // 16])
+            )
+
+        def product(b, h):
+            cols = slice(h * HALF, (h + 1) * HALF)
+            acc = psum.tile([P, HALF], F32, name=f"acc{b}{h}")
+            nc.tensor.matmul_mx(
+                out=acc[:],
+                lhsT=w_c[b][:].bitcast(FP8X4),
+                lhsT_scale=w_s[b][:],
+                rhs=x_c[:, cols].bitcast(FP8X4),
+                rhs_scale=x_s[:, cols],
+                start=True,
+                stop=True,
+            )
+            if b == 1:
+                nc.vector.tensor_scalar(y[b][:, cols], acc[:], WING, None, MULT)
+            else:
+                nc.scalar.activation(y[b][:, cols], acc[:], COPY, scale=WING)
+
+        nc.vector.tensor_copy(x_s[:], table_scales[:].indirect(offs_t[:]))
+        cast(0)
+        quantize(0)
+        pick_words(0)
+        cast(1)
+        product(0, 0)
+        pick_words(1)
+        product(0, 1)
+        quantize(1)
+        product(1, 0)
+        product(1, 1)
+
+        def fresh(name, width):
+            return [held.tile([P, width], F32, name=f"{name}{b}") for b in range(BLOCKS)]
+
+        end_a, ends, wing_a, wings, edge = (fresh(n, V) for n in ("end_a", "ends", "wing_a", "wings", "edge"))
+        own, part, res = (fresh(n, R) for n in ("own", "part", "res"))
+
+        def first_halves(b):
+            nc.scalar.activation(end_a[b][:], y[b][:].indirect(ea_t[:]), COPY)
+            nc.scalar.activation(wing_a[b][:], y[b][:].indirect(wa_t[:]), COPY)
+
+        def add_ends(b):
+            nc.vector.tensor_tensor(ends[b][:], y[b][:].indirect(eb_t[:]), end_a[b][:], ADD)
+
+        def add_wings(b):
+            nc.vector.tensor_tensor(wings[b][:], y[b][:].indirect(wb_t[:]), wing_a[b][:], ADD)
+
+        def make_edge(b):
+            nc.vector.scalar_tensor_tensor(edge[b][:], ends[b][:], END_TO_WING, wings[b][:], MULT, ADD)
+
+        def fetch_own(b):
+            nc.scalar.activation(own[b][:], y[b][:].indirect(cen_t[:]), COPY, scale=OWN_TO_WING)
+
+        def add_first(b):
+            nc.vector.tensor_tensor(part[b][:], edge[b][:].indirect(i1_t[:]), own[b][:], ADD)
+
+        def add_second(b):
+            nc.vector.tensor_tensor(res[b][:], edge[b][:].indirect(i2_t[:]), part[b][:], ADD)
+            nc.sync.dma_start(out[b * P : (b + 1) * P, :], res[b][:])
+
+        first_halves(0)
+        first_halves(1)
+        fetch_own(0)
+        fetch_own(1)
+        add_ends(0)
+        add_wings(0)
+        add_ends(1)
+        make_edge(0)
+        add_wings(1)
+        add_first(0)
+        make_edge(1)
+        add_second(0)
+        add_first(1)
+        add_second(1)

@@ -80,56 +80,49 @@ def tile_picked_yloopsd_one_p_kernel(
                 in_=w_bf[b][:].rearrange("p n j -> p (n j)"),
             )
 
-        def pick_words(h):
-            cols = slice(h * HALF, (h + 1) * HALF)
-            nc.vector.tensor_copy(
-                x_c[:, cols], table_words[:].indirect(offs_t[:, h * HALF // 16 : (h + 1) * HALF // 16])
-            )
+        def pick_words(lo, hi):
+            nc.vector.tensor_copy(x_c[:, lo:hi], table_words[:].indirect(offs_t[:, lo // 16 : hi // 16]))
 
-        def product(b, h):
-            cols = slice(h * HALF, (h + 1) * HALF)
-            acc = psum.tile([P, HALF], F32, name=f"acc{b}{h}")
+        def product(b, lo, hi):
+            acc = psum.tile([P, hi - lo], F32, name=f"acc{b}_{lo}")
             nc.tensor.matmul_mx(
                 out=acc[:],
                 lhsT=w_c[b][:].bitcast(FP8X4),
                 lhsT_scale=w_s[b][:],
-                rhs=x_c[:, cols].bitcast(FP8X4),
-                rhs_scale=x_s[:, cols],
+                rhs=x_c[:, lo:hi].bitcast(FP8X4),
+                rhs_scale=x_s[:, lo:hi],
                 start=True,
                 stop=True,
             )
-            if b == 1:
-                nc.vector.tensor_scalar(y[b][:, cols], acc[:], WING, None, MULT)
+            if b == 1 or lo == 0:
+                nc.vector.tensor_scalar(y[b][:, lo:hi], acc[:], WING, None, MULT)
             else:
-                nc.scalar.activation(y[b][:, cols], acc[:], COPY, scale=WING)
+                nc.scalar.activation(y[b][:, lo:hi], acc[:], COPY, scale=WING)
 
         nc.vector.tensor_copy(x_s[:], table_scales[:].indirect(offs_t[:]))
         cast(0)
         quantize(0)
-        pick_words(0)
         cast(1)
-        product(0, 0)
-        pick_words(1)
-        product(0, 1)
+        for lo, hi in ((0, 256), (256, 384), (384, 512)):
+            pick_words(lo, hi)
+            product(0, lo, hi)
         quantize(1)
-        product(1, 0)
-        product(1, 1)
 
         def fresh(name, width):
             return [held.tile([P, width], F32, name=f"{name}{b}") for b in range(BLOCKS)]
 
-        end_a, ends, wing_a, wings, edge = (fresh(n, V) for n in ("end_a", "ends", "wing_a", "wings", "edge"))
-        own, part, res = (fresh(n, R) for n in ("own", "part", "res"))
+        end_a, ends, wing_a, wings = (fresh(n, V) for n in ("end_a", "ends", "wing_a", "wings"))
+        edge = [wing_a[1], wing_a[0]]
+        own, part, res, first = (fresh(n, R) for n in ("own", "part", "res", "first"))
 
-        def first_halves(b):
+        def fetch_end(b):
             nc.scalar.activation(end_a[b][:], y[b][:].indirect(ea_t[:]), COPY)
-            nc.scalar.activation(wing_a[b][:], y[b][:].indirect(wa_t[:]), COPY)
-
-        def add_ends(b):
-            nc.vector.tensor_tensor(ends[b][:], y[b][:].indirect(eb_t[:]), end_a[b][:], ADD)
 
         def add_wings(b):
             nc.vector.tensor_tensor(wings[b][:], y[b][:].indirect(wb_t[:]), wing_a[b][:], ADD)
+
+        def add_ends(b):
+            nc.vector.tensor_tensor(ends[b][:], y[b][:].indirect(eb_t[:]), end_a[b][:], ADD)
 
         def make_edge(b):
             nc.vector.scalar_tensor_tensor(edge[b][:], ends[b][:], END_TO_WING, wings[b][:], MULT, ADD)
@@ -137,24 +130,26 @@ def tile_picked_yloopsd_one_p_kernel(
         def fetch_own(b):
             nc.scalar.activation(own[b][:], y[b][:].indirect(cen_t[:]), COPY, scale=OWN_TO_WING)
 
-        def add_first(b):
-            nc.vector.tensor_tensor(part[b][:], edge[b][:].indirect(i1_t[:]), own[b][:], ADD)
+        def fetch_first(b):
+            nc.scalar.activation(first[b][:], edge[b][:].indirect(i1_t[:]), COPY)
 
         def add_second(b):
-            nc.vector.tensor_tensor(res[b][:], edge[b][:].indirect(i2_t[:]), part[b][:], ADD)
+            nc.vector.tensor_tensor(part[b][:], edge[b][:].indirect(i2_t[:]), own[b][:], ADD)
+
+        def finish(b):
+            nc.vector.tensor_tensor(res[b][:], part[b][:], first[b][:], ADD)
             nc.sync.dma_start(out[b * P : (b + 1) * P, :], res[b][:])
 
-        first_halves(0)
-        first_halves(1)
-        fetch_own(0)
-        fetch_own(1)
+        fetch_end(0)
+        nc.scalar.activation(wing_a[0][:], y[0][:].indirect(wa_t[:]), COPY)
+        product(1, 0, 256)
+        product(1, 256, 512)
+        nc.scalar.activation(wing_a[1][:], y[1][:].indirect(wa_t[:]), COPY)
+        fetch_end(1)
         add_ends(0)
         add_wings(0)
-        add_ends(1)
-        make_edge(0)
         add_wings(1)
-        add_first(0)
-        make_edge(1)
-        add_second(0)
-        add_first(1)
-        add_second(1)
+        add_ends(1)
+        for step in (fetch_own, make_edge, fetch_first, add_second, finish):
+            for b in range(BLOCKS):
+                step(b)

@@ -68,10 +68,8 @@ def tile_picked_yloopsd_one_p_kernel(
         w_s = [held.tile([P, P], U8, name=f"w_s{b}", align_bytes=64) for b in range(BLOCKS)]
         y = [held.tile([P, S], F32, name=f"y{b}") for b in range(BLOCKS)]
 
-        def cast(b):
-            nc.scalar.activation(
-                w_bf[b][:], w_raw[b][:].rearrange("p j n -> p n j"), COPY
-            )
+        def rows_of(b, lo, hi):
+            return w_raw[b][:, :, lo:hi].rearrange("p j n -> p n j")
 
         def quantize(b):
             nc.vector.quantize_mx(
@@ -94,15 +92,15 @@ def tile_picked_yloopsd_one_p_kernel(
                 start=True,
                 stop=True,
             )
-            if b == 1 or lo == 0:
+            if (b, lo) == (1, 256):
                 nc.vector.tensor_scalar(y[b][:, lo:hi], acc[:], WING, None, MULT)
             else:
                 nc.scalar.activation(y[b][:, lo:hi], acc[:], COPY, scale=WING)
 
         nc.vector.tensor_copy(x_s[:], table_scales[:].indirect(offs_t[:]))
-        cast(0)
+        nc.vector.tensor_copy(w_bf[0][:], rows_of(0, 0, 128))
         quantize(0)
-        cast(1)
+        nc.scalar.activation(w_bf[1][:], rows_of(1, 0, 128), COPY)
         for lo, hi in ((0, 256), (256, 384), (384, 512)):
             pick_words(lo, hi)
             product(0, lo, hi)
@@ -141,7 +139,7 @@ def tile_picked_yloopsd_one_p_kernel(
             nc.sync.dma_start(out[b * P : (b + 1) * P, :], res[b][:])
 
         fetch_end(0)
-        nc.scalar.activation(wing_a[0][:], y[0][:].indirect(wa_t[:]), COPY)
+        nc.vector.tensor_copy(wing_a[0][:], y[0][:].indirect(wa_t[:]))
         product(1, 0, 256)
         product(1, 256, 512)
         nc.scalar.activation(wing_a[1][:], y[1][:].indirect(wa_t[:]), COPY)

from contextlib import ExitStack

import concourse.mybir as mybir

K, T, S, N, V, R = 512, 1024, 512, 256, 256, 128
FLOPS = 2 * K * N * S

F32 = mybir.dt.float32
BF16 = mybir.dt.bfloat16
I32 = mybir.dt.int32
U32 = mybir.dt.uint32
U16 = mybir.dt.uint16
U8 = mybir.dt.uint8
FP8X4 = mybir.dt.float8_e4m3fn_x4
ADD = mybir.AluOpType.add
MULT = mybir.AluOpType.mult
COPY = mybir.ActivationFunctionType.Copy

P = 128
PACK = 4
BLOCKS = N // P
HALF = S // 2
WING = 0.3 * 0.125
END_TO_WING = 0.375 / 0.125
OWN_TO_WING = 0.4 / WING


def tile_picked_yloopsd_one_p_kernel(
    tc, x_words, x_scales, w1, offs, ea, eb, wa, wb, cen, i1, i2, out
):
    nc = tc.nc
    with ExitStack() as ctx:
        held = ctx.enter_context(tc.tile_pool(name="held", bufs=1))
        psum = ctx.enter_context(tc.psum_pool(name="psum", bufs=1))

        def load_list(name, source):
            tile = held.tile([P, source.shape[1]], U16, name=name)
            nc.sync.dma_start(tile[:], source)
            return tile

        table_scales = held.tile([P, T], U8, align_bytes=64)
        offs_t = load_list("offs_t", offs)
        for q in range(4):
            (nc.sync if q < 2 else nc.scalar).dma_start(
                table_scales[32 * q : 32 * q + 32, :].bitcast(I32),
                x_scales[0, 4 * q : 4 * q + 4, :].bitcast(I32).unsqueeze(0).to_broadcast([8, 4, T // 4]),
            )
        w_rows = w1.rearrange("(p j) n -> p j n", j=PACK)
        w_raw = [held.tile([P, PACK, P], F32, name=f"w_raw{b}", align_bytes=64) for b in range(BLOCKS)]
        nc.sync.dma_start(w_raw[0][:], w_rows[:, :, 0:P])
        table_words = held.tile([P, T], U32, align_bytes=64)
        nc.sync.dma_start(
            table_words[:].bitcast(I32), x_words[0].rearrange("p n t -> p (n t)").bitcast(I32)
        )
        nc.sync.dma_start(w_raw[1][:], w_rows[:, :, P : 2 * P])
        ea_t = load_list("ea_t", ea)
        wa_t = load_list("wa_t", wa)
        eb_t = load_list("eb_t", eb)
        wb_t = load_list("wb_t", wb)
        cen_t = load_list("cen_t", cen)
        i1_t = load_list("i1_t", i1)
        i2_t = load_list("i2_t", i2)

        x_s = held.tile([P, S], U8, align_bytes=64)
        x_c = held.tile([P, S], U32, align_bytes=64)
        w_bf = [held.tile([P, P, PACK], BF16, name=f"w_bf{b}", align_bytes=64) for b in range(BLOCKS)]
        w_c = [held.tile([P, P], U32, name=f"w_c{b}", align_bytes=64) for b in range(BLOCKS)]
        w_s = [held.tile([P, P], U8, name=f"w_s{b}", align_bytes=64) for b in range(BLOCKS)]
        y = [held.tile([P, S], F32, name=f"y{b}") for b in range(BLOCKS)]

        def rows_of(b, lo, hi):
            return w_raw[b][:, :, lo:hi].rearrange("p j n -> p n j")

        def quantize(b):
            nc.vector.quantize_mx(
                out=w_c[b][:].bitcast(FP8X4),
                scales=w_s[b][:],
                in_=w_bf[b][:].rearrange("p n j -> p (n j)"),
            )

        def pick_words(lo, hi):
            nc.vector.tensor_copy(x_c[:, lo:hi], table_words[:].indirect(offs_t[:, lo // 16 : hi // 16]))

        def product(b, lo, hi):
            acc = psum.tile([P, hi - lo], F32, name=f"acc{b}_{lo}")
            nc.tensor.matmul_mx(
                out=acc[:],
                lhsT=w_c[b][:].bitcast(FP8X4),
                lhsT_scale=w_s[b][:],
                rhs=x_c[:, lo:hi].bitcast(FP8X4),
                rhs_scale=x_s[:, lo:hi],
                start=True,
                stop=True,
            )
            if (b, lo) == (1, 256):
                nc.vector.tensor_scalar(y[b][:, lo:hi], acc[:], WING, None, MULT)
            else:
                nc.scalar.activation(y[b][:, lo:hi], acc[:], COPY, scale=WING)

        nc.vector.tensor_copy(x_s[:], table_scales[:].indirect(offs_t[:]))
        nc.vector.tensor_copy(w_bf[0][:], rows_of(0, 0, 128))
        quantize(0)
        nc.scalar.activation(w_bf[1][:], rows_of(1, 0, 128), COPY)
        for lo, hi in ((0, 256), (256, 384), (384, 512)):
            pick_words(lo, hi)
            product(0, lo, hi)
        quantize(1)

        def fresh(name, width):
            return [held.tile([P, width], F32, name=f"{name}{b}") for b in range(BLOCKS)]

        end_a, ends, wing_a, wings = (fresh(n, V) for n in ("end_a", "ends", "wing_a", "wings"))
        edge = [wing_a[1], wing_a[0]]
        own, part, res, first = (fresh(n, R) for n in ("own", "part", "res", "first"))

        def fetch_end(b):
            nc.scalar.activation(end_a[b][:], y[b][:].indirect(ea_t[:]), COPY)

        def add_wings(b):
            nc.vector.tensor_tensor(wings[b][:], y[b][:].indirect(wb_t[:]), wing_a[b][:], ADD)

        def add_ends(b):
            nc.vector.tensor_tensor(ends[b][:], y[b][:].indirect(eb_t[:]), end_a[b][:], ADD)

        def make_edge(b):
            nc.vector.scalar_tensor_tensor(edge[b][:], ends[b][:], END_TO_WING, wings[b][:], MULT, ADD)

        def fetch_own(b):
            nc.scalar.activation(own[b][:], y[b][:].indirect(cen_t[:]), COPY, scale=OWN_TO_WING)

        def fetch_first(b):
            nc.scalar.activation(first[b][:], edge[b][:].indirect(i1_t[:]), COPY)

        def add_second(b):
            nc.vector.tensor_tensor(part[b][:], edge[b][:].indirect(i2_t[:]), own[b][:], ADD)

        def finish(b):
            nc.vector.tensor_tensor(res[b][:], part[b][:], first[b][:], ADD)
            nc.sync.dma_start(out[b * P : (b + 1) * P, :], res[b][:])

        fetch_end(0)
        nc.vector.tensor_copy(wing_a[0][:], y[0][:].indirect(wa_t[:]))
        product(1, 0, 256)
        product(1, 256, 512)
        nc.scalar.activation(wing_a[1][:], y[1][:].indirect(wa_t[:]), COPY)
        fetch_end(1)
        add_ends(0)
        add_wings(0)
        add_wings(1)
        add_ends(1)
        for step in (fetch_own, make_edge, fetch_first, add_second, finish):
            for b in range(BLOCKS):
                step(b)
